import numpy as np
import ml_dtypes


def mxq(x, axis, fmt="e4m3"):
    dtype, down = {"e4m3": (ml_dtypes.float8_e4m3fn, 7), "e5m2": (ml_dtypes.float8_e5m2, 14)}[fmt]
    v = np.moveaxis(np.asarray(x, np.float32).astype(ml_dtypes.bfloat16).astype(np.float64), axis, -1)
    blocks = v.reshape(v.shape[:-1] + (-1, 32))
    amax = np.abs(blocks).max(-1, keepdims=True)
    byte = np.maximum(np.where(amax > 0, np.frexp(amax)[1] - 1 + 127, 0) - down, 1)
    scale = np.exp2(byte - 127.0)
    codes = (blocks / scale).astype(np.float32).astype(dtype).astype(np.float64)
    return np.moveaxis((codes * scale).reshape(v.shape), -1, axis)


WIDE = False


def mx_kscale(k):
    if not WIDE:
        return np.ones(k)
    levels = np.array([10, -10, 5, -5, 0])
    if k % 512:
        return np.exp2(np.random.permutation(np.resize(levels, k // 32))).repeat(32)
    a = np.empty((k // 512, 16))
    for p in range(k // 512):
        a[p, :8] = np.random.permutation(np.resize(levels, 8))
        for g in range(8):
            far = levels[np.abs(levels - a[p, g]) >= 10]
            a[p, g + 8] = far[np.random.randint(len(far))]
    return np.exp2(a.ravel()).repeat(32)


def f64(x):
    return np.asarray(x).astype(np.float64)


def striped(idx):
    return np.tile(idx.reshape(-1, 16).T, (8, 1)).astype(np.uint16)


def unstriped(offs):
    return offs[:16].T.reshape(-1).astype(np.int64)


K, T, E, C, N = 512, 4096, 16, 256, 128


def by_expert(wq, xq):
    return np.concatenate([wq[e].T @ xq[:, e * C:(e + 1) * C] for e in range(E)], axis=1)


def setup_inputs():
    n = np.random.standard_normal
    s = mx_kscale(K)[:, None]
    return {
        "xT": (n((K, T)) * s).astype(np.float32),
        "w": (n((E, K, N)) / np.sqrt(K) / s[None]).astype(np.float32),
        "gate": np.tile(np.random.uniform(0.2, 1.0, E * C), (N, 1)).astype(np.float32),
        "offs": striped(np.random.permutation(T)[:E * C]),
    }


def reference(xT, w, gate, offs):
    idx = unstriped(offs)
    xq = mxq(f64(xT)[:, idx], 0, "e4m3")
    y = by_expert(mxq(f64(w), 1, "e4m3"), xq)
    out = np.zeros((N, T))
    out[:, idx] = f64(gate) * y
    return out

@@ -1,0 +1,115 @@
+from contextlib import ExitStack
+
+import concourse.mybir as mybir
+
+K, T, E, C, N = 512, 4096, 16, 256, 128
+FLOPS = 2 * K * N * E * C
+
+F32 = mybir.dt.float32
+BF16 = mybir.dt.bfloat16
+U32 = mybir.dt.uint32
+U16 = mybir.dt.uint16
+U8 = mybir.dt.uint8
+FP8X4 = mybir.dt.float8_e4m3fn_x4
+MULT = mybir.AluOpType.mult
+
+P = 128
+SLOTS = E * C
+TOK = 512
+GATHER = 2048
+QUANT = 1024
+WE = 4
+SCAT = 1024
+VEC_HALF0 = (1, 3, 5, 7)
+VEC_HALF1 = (7,)
+
+
+def tile_routed_moe_kernel(tc, xT, w, gate, offs, out):
+    nc = tc.nc
+    with ExitStack() as ctx:
+        keep = ctx.enter_context(tc.tile_pool(name="keep", bufs=1))
+        xraw = ctx.enter_context(tc.tile_pool(name="xraw", bufs=10))
+        wraw = ctx.enter_context(tc.tile_pool(name="wraw", bufs=4))
+        wstage = ctx.enter_context(tc.tile_pool(name="wstage", bufs=3))
+        psum = ctx.enter_context(tc.psum_pool(name="psum", bufs=8))
+
+        offsets = keep.tile([P, SLOTS // 16], U16)
+        nc.sync.dma_start(offsets[:], offs)
+
+        pairs = [keep.tile([P, T, 2], BF16, align_bytes=64, name="pairs%d" % u) for u in (0, 1)]
+        grp = [keep.tile([P, GATHER, 4], BF16, align_bytes=64, name="grp%d" % g) for g in range(SLOTS // GATHER)]
+        planes = xT.rearrange("(p t) n -> p t n", t=4)
+        for u, vec in ((0, VEC_HALF0), (1, VEC_HALF1)):
+            for c in range(T // TOK):
+                cols = slice(c * TOK, (c + 1) * TOK)
+                raw = xraw.tile([P, 2, TOK], F32)
+                nc.sync.dma_start(raw[:], planes[:, 2 * u : 2 * u + 2, cols])
+                src = raw[:].rearrange("p t n -> p n t")
+                if c in vec:
+                    nc.vector.tensor_copy(pairs[u][:, cols, :], src)
+                else:
+                    nc.scalar.copy(pairs[u][:, cols, :], src)
+            words = pairs[u][:].rearrange("p n t -> p (n t)").bitcast(U32)
+            for g in range(SLOTS // GATHER):
+                idx = offsets[:, g * GATHER // 16 : (g + 1) * GATHER // 16]
+                dst = grp[g][:].rearrange("p n j -> p (n j)").bitcast(U32)
+                nc.vector.tensor_copy(dst[:, u::2], words.indirect(idx))
+
+        codes = []
+        scales = []
+        for q in range(SLOTS // QUANT):
+            cq = keep.tile([P, QUANT], U32, align_bytes=64, name="codes%d" % q)
+            sq = keep.tile([P, QUANT], U8, align_bytes=64, name="scales%d" % q)
+            off = q * QUANT % GATHER
+            nc.vector.quantize_mx(
+                out=cq[:].bitcast(FP8X4),
+                scales=sq[:],
+                in_=grp[q * QUANT // GATHER][:, off : off + QUANT, :].rearrange("p n j -> p (n j)"),
+            )
+            codes.append(cq)
+            scales.append(sq)
+
+        wcodes = []
+        wscales = []
+        rows = w.rearrange("e (p j) n -> p e (j n)", j=4)
+        for i in range(E // WE):
+            raw = wraw.tile([P, WE, 4 * N], F32, name="wr")
+            nc.sync.dma_start(raw[:], rows[:, i * WE : (i + 1) * WE, :])
+            st = wstage.tile([P, WE, N, 4], BF16, align_bytes=64)
+            nc.scalar.copy(st[:], raw[:].rearrange("p e (j n) -> p e n j", j=4))
+            wc = keep.tile([P, WE * N], U32, align_bytes=64, name="wcodes%d" % i)
+            ws = keep.tile([P, WE * N], U8, align_bytes=64, name="wscales%d" % i)
+            nc.vector.quantize_mx(out=wc[:].bitcast(FP8X4), scales=ws[:], in_=st[:].rearrange("p e n j -> p (e n j)"))
+            wcodes.append(wc)
+            wscales.append(ws)
+
+        gates = []
+        for s in range(SLOTS // SCAT):
+            gt = keep.tile([P, SCAT], F32, name="gate%d" % s)
+            nc.sync.dma_start(gt[:], gate[:, s * SCAT : (s + 1) * SCAT])
+            gates.append(gt)
+
+        window = keep.tile([P, T], F32)
+        for s in range(SLOTS // SCAT):
+            sums = keep.tile([P, SCAT], F32, name="sums%d" % s)
+            for b in range(SCAT // 512):
+                bank = psum.tile([P, 512], F32)
+                for h in range(512 // C):
+                    slot = s * SCAT + b * 512 + h * C
+                    e = slot // C
+                    q, qo = slot // QUANT, slot % QUANT
+                    wo = e % WE * N
+                    nc.tensor.matmul_mx(
+                        out=bank[:, h * C : (h + 1) * C],
+                        lhsT=wcodes[e // WE][:, wo : wo + N].bitcast(FP8X4),
+                        lhsT_scale=wscales[e // WE][:, wo : wo + N],
+                        rhs=codes[q][:, qo : qo + C].bitcast(FP8X4),
+                        rhs_scale=scales[q][:, qo : qo + C],
+                        start=True,
+                        stop=True,
+                    )
+                nc.scalar.copy(sums[:, b * 512 : (b + 1) * 512], bank[:])
+            idx = offsets[:, s * SCAT // 16 : (s + 1) * SCAT // 16]
+            nc.vector.tensor_tensor(window[:].indirect(idx), sums[:], gates[s][:], MULT)
+
+        nc.sync.dma_start(out, window[:])

@@ -12,104 +12,146 @@ U16 = mybir.dt.uint16
 U8 = mybir.dt.uint8
 FP8X4 = mybir.dt.float8_e4m3fn_x4
 MULT = mybir.AluOpType.mult
+ADD = mybir.AluOpType.add
 
 P = 128
 SLOTS = E * C
-TOK = 512
-GATHER = 2048
+CHUNKS = (
+    (
+        (1024, ((512, False), (512, True))),
+        (1024, ((512, False), (512, True))),
+        (1024, ((512, False), (512, True))),
+        (512, ((256, False), (256, True))),
+        (512, ((256, False), (256, True))),
+    ),
+    (
+        (1024, ((1024, False),)),
+        (1024, ((1024, False),)),
+        (1024, ((1024, False),)),
+        (512, ((512, False),)),
+        (512, ((512, True),)),
+    ),
+)
+GATHERS = ((0, 1024), (1024, 1024), (2048, 2048))
 QUANT = 1024
+SPREAD = 512
 WE = 4
 SCAT = 1024
-VEC_HALF0 = (1, 3, 5, 7)
-VEC_HALF1 = (7,)
+BANK = 512
 
 
 def tile_routed_moe_kernel(tc, xT, w, gate, offs, out):
     nc = tc.nc
     with ExitStack() as ctx:
         keep = ctx.enter_context(tc.tile_pool(name="keep", bufs=1))
-        xraw = ctx.enter_context(tc.tile_pool(name="xraw", bufs=10))
-        wraw = ctx.enter_context(tc.tile_pool(name="wraw", bufs=4))
-        wstage = ctx.enter_context(tc.tile_pool(name="wstage", bufs=3))
+        rawp = ctx.enter_context(tc.tile_pool(name="rawp", bufs=6))
+        turns = ctx.enter_context(tc.tile_pool(name="turns", bufs=1))
         psum = ctx.enter_context(tc.psum_pool(name="psum", bufs=8))
 
         offsets = keep.tile([P, SLOTS // 16], U16)
         nc.sync.dma_start(offsets[:], offs)
 
         pairs = [keep.tile([P, T, 2], BF16, align_bytes=64, name="pairs%d" % u) for u in (0, 1)]
-        grp = [keep.tile([P, GATHER, 4], BF16, align_bytes=64, name="grp%d" % g) for g in range(SLOTS // GATHER)]
+        apart = []
+        for first, n in GATHERS:
+            a = keep.tile([P, 2, n, 2], BF16, align_bytes=64, name="apart%d" % first)
+            apart.append(a)
         planes = xT.rearrange("(p t) n -> p t n", t=4)
-        for u, vec in ((0, VEC_HALF0), (1, VEC_HALF1)):
-            for c in range(T // TOK):
-                cols = slice(c * TOK, (c + 1) * TOK)
-                raw = xraw.tile([P, 2, TOK], F32)
-                nc.sync.dma_start(raw[:], planes[:, 2 * u : 2 * u + 2, cols])
-                src = raw[:].rearrange("p t n -> p n t")
-                if c in vec:
-                    nc.vector.tensor_copy(pairs[u][:, cols, :], src)
-                else:
-                    nc.scalar.copy(pairs[u][:, cols, :], src)
+        for u in (0, 1):
+            start = 0
+            for width, pieces in CHUNKS[u]:
+                raw = rawp.tile([P, 2, width], F32, name="raw")
+                nc.sync.dma_start(raw[:], planes[:, 2 * u : 2 * u + 2, start : start + width])
+                done = 0
+                for n, on_vector in pieces:
+                    dst = pairs[u][:, start + done : start + done + n, :]
+                    src = raw[:, :, done : done + n].rearrange("p t n -> p n t")
+                    if on_vector:
+                        nc.vector.tensor_copy(dst, src)
+                    else:
+                        nc.scalar.copy(dst, src)
+                    done += n
+                start += width
             words = pairs[u][:].rearrange("p n t -> p (n t)").bitcast(U32)
-            for g in range(SLOTS // GATHER):
-                idx = offsets[:, g * GATHER // 16 : (g + 1) * GATHER // 16]
-                dst = grp[g][:].rearrange("p n j -> p (n j)").bitcast(U32)
-                nc.vector.tensor_copy(dst[:, u::2], words.indirect(idx))
+            for (first, n), a in zip(GATHERS, apart):
+                nc.vector.tensor_copy(
+                    a[:, u, :, :].rearrange("p n i -> p (n i)").bitcast(U32),
+                    words.indirect(offsets[:, first // 16 : (first + n) // 16]),
+                )
 
-        codes = []
-        scales = []
-        for q in range(SLOTS // QUANT):
+        def spread(grouped, a, first):
+            nc.scalar.copy(
+                grouped.rearrange("p n (u i) -> p n u i", u=2),
+                a[:, :, first : first + SPREAD, :].rearrange("p u n i -> p n u i"),
+            )
+
+        def quantize(q, grouped):
             cq = keep.tile([P, QUANT], U32, align_bytes=64, name="codes%d" % q)
             sq = keep.tile([P, QUANT], U8, align_bytes=64, name="scales%d" % q)
-            off = q * QUANT % GATHER
-            nc.vector.quantize_mx(
-                out=cq[:].bitcast(FP8X4),
-                scales=sq[:],
-                in_=grp[q * QUANT // GATHER][:, off : off + QUANT, :].rearrange("p n j -> p (n j)"),
-            )
-            codes.append(cq)
-            scales.append(sq)
+            nc.vector.quantize_mx(out=cq[:].bitcast(FP8X4), scales=sq[:], in_=grouped.rearrange("p n j -> p (n j)"))
+            return cq, sq
+
+        codes = {}
+        for q in (0, 1):
+            grouped = keep.tile([P, QUANT, 4], BF16, align_bytes=64, name="grouped%d" % q)
+            for s in range(0, QUANT, SPREAD):
+                spread(grouped[:, s : s + SPREAD, :], apart[q], s)
+            codes[q] = quantize(q, grouped[:])
 
         wcodes = []
         wscales = []
+        wst = turns.tile([P, E, N, 4], BF16, align_bytes=64, name="big")
         rows = w.rearrange("e (p j) n -> p e (j n)", j=4)
         for i in range(E // WE):
-            raw = wraw.tile([P, WE, 4 * N], F32, name="wr")
+            raw = rawp.tile([P, WE, 4 * N], F32, name="raw")
             nc.sync.dma_start(raw[:], rows[:, i * WE : (i + 1) * WE, :])
-            st = wstage.tile([P, WE, N, 4], BF16, align_bytes=64)
-            nc.scalar.copy(st[:], raw[:].rearrange("p e (j n) -> p e n j", j=4))
+            st = wst[:, i * WE : (i + 1) * WE, :, :]
+            nc.gpsimd.tensor_scalar(st, raw[:].rearrange("p e (j n) -> p e n j", j=4), 1.0, 0.0, MULT, ADD)
             wc = keep.tile([P, WE * N], U32, align_bytes=64, name="wcodes%d" % i)
             ws = keep.tile([P, WE * N], U8, align_bytes=64, name="wscales%d" % i)
-            nc.vector.quantize_mx(out=wc[:].bitcast(FP8X4), scales=ws[:], in_=st[:].rearrange("p e n j -> p (e n j)"))
+            nc.vector.quantize_mx(out=wc[:].bitcast(FP8X4), scales=ws[:], in_=st.rearrange("p e n j -> p (e n j)"))
             wcodes.append(wc)
             wscales.append(ws)
 
-        gates = []
-        for s in range(SLOTS // SCAT):
-            gt = keep.tile([P, SCAT], F32, name="gate%d" % s)
-            nc.sync.dma_start(gt[:], gate[:, s * SCAT : (s + 1) * SCAT])
-            gates.append(gt)
+        gates = keep.tile([P, SLOTS], F32)
+        for s in range(0, SLOTS, SCAT):
+            nc.sync.dma_start(gates[:, s : s + SCAT], gate[:, s : s + SCAT])
 
-        window = keep.tile([P, T], F32)
-        for s in range(SLOTS // SCAT):
-            sums = keep.tile([P, SCAT], F32, name="sums%d" % s)
-            for b in range(SCAT // 512):
-                bank = psum.tile([P, 512], F32)
-                for h in range(512 // C):
-                    slot = s * SCAT + b * 512 + h * C
-                    e = slot // C
-                    q, qo = slot // QUANT, slot % QUANT
-                    wo = e % WE * N
-                    nc.tensor.matmul_mx(
-                        out=bank[:, h * C : (h + 1) * C],
-                        lhsT=wcodes[e // WE][:, wo : wo + N].bitcast(FP8X4),
-                        lhsT_scale=wscales[e // WE][:, wo : wo + N],
-                        rhs=codes[q][:, qo : qo + C].bitcast(FP8X4),
-                        rhs_scale=scales[q][:, qo : qo + C],
-                        start=True,
-                        stop=True,
-                    )
-                nc.scalar.copy(sums[:, b * 512 : (b + 1) * 512], bank[:])
-            idx = offsets[:, s * SCAT // 16 : (s + 1) * SCAT // 16]
-            nc.vector.tensor_tensor(window[:].indirect(idx), sums[:], gates[s][:], MULT)
+        window = turns.tile([P, T], F32, align_bytes=64, name="big")
+
+        def multiply(b):
+            bank = psum.tile([P, BANK], F32)
+            for slot in range(b, b + BANK, C):
+                e, q, qo = slot // C, slot // QUANT, slot % QUANT
+                wo = e % WE * N
+                nc.tensor.matmul_mx(
+                    out=bank[:, slot - b : slot - b + C],
+                    lhsT=wcodes[e // WE][:, wo : wo + N].bitcast(FP8X4),
+                    lhsT_scale=wscales[e // WE][:, wo : wo + N],
+                    rhs=codes[q][0][:, qo : qo + C].bitcast(FP8X4),
+                    rhs_scale=codes[q][1][:, qo : qo + C],
+                    start=True,
+                    stop=True,
+                )
+            return bank
+
+        def scatter(start, banks, sums):
+            for b, bank in enumerate(banks):
+                nc.scalar.copy(sums[:, b * BANK : (b + 1) * BANK], bank[:])
+            n = len(banks) * BANK
+            idx = offsets[:, start // 16 : (start + n) // 16]
+            nc.vector.tensor_tensor(window[:].indirect(idx), sums[:], gates[:, start : start + n], MULT)
+
+        sums0 = turns.tile([P, 512], F32, align_bytes=64, name="early")
+        scatter(0, [multiply(0)], sums0)
+        sums1 = keep.tile([P, 1536], F32)
+        scatter(512, [multiply(512), multiply(1024), multiply(1536)], sums1)
+        late = turns.tile([P, 2048, 4], BF16, align_bytes=64, name="early")
+        for s in (0, 1024, 1536, 512):
+            spread(late[:, s : s + SPREAD, :], apart[2], s)
+        for q in (3, 2):
+            codes[q] = quantize(q, late[:, (q - 2) * QUANT : (q - 1) * QUANT, :])
+            sums = keep.tile([P, SCAT], F32, name="sums%d" % q)
+            scatter(q * SCAT, [multiply(q * SCAT), multiply(q * SCAT + BANK)], sums)
 
         nc.sync.dma_start(out, window[:])

@@ -13,6 +13,7 @@ U8 = mybir.dt.uint8
 FP8X4 = mybir.dt.float8_e4m3fn_x4
 MULT = mybir.AluOpType.mult
 ADD = mybir.AluOpType.add
+IDENTITY = mybir.ActivationFunctionType.Identity
 
 P = 128
 SLOTS = E * C
@@ -52,9 +53,11 @@ def tile_routed_moe_kernel(tc, xT, w, gate, offs, out):
         nc.sync.dma_start(offsets[:], offs)
 
         pairs = [keep.tile([P, T, 2], BF16, align_bytes=64, name="pairs%d" % u) for u in (0, 1)]
+        zero = turns.tile([P, 1], F32, align_bytes=64, name="early")
+        nc.gpsimd.memset(zero[:], 0.0)
         apart = []
         for first, n in GATHERS:
-            a = keep.tile([P, 2, n, 2], BF16, align_bytes=64, name="apart%d" % first)
+            a = turns.tile([P, 2, n, 2], BF16, align_bytes=64, name="apart%d" % first)
             apart.append(a)
         planes = xT.rearrange("(p t) n -> p t n", t=4)
         for u in (0, 1):
@@ -138,19 +141,26 @@ def tile_routed_moe_kernel(tc, xT, w, gate, offs, out):
         def scatter(start, banks, sums):
             for b, bank in enumerate(banks):
                 nc.scalar.copy(sums[:, b * BANK : (b + 1) * BANK], bank[:])
-            n = len(banks) * BANK
+            put_back(start, len(banks) * BANK, sums)
+
+        def put_back(start, n, sums):
             idx = offsets[:, start // 16 : (start + n) // 16]
             nc.vector.tensor_tensor(window[:].indirect(idx), sums[:], gates[:, start : start + n], MULT)
 
-        sums0 = turns.tile([P, 512], F32, align_bytes=64, name="early")
-        scatter(0, [multiply(0)], sums0)
-        sums1 = keep.tile([P, 1536], F32)
-        scatter(512, [multiply(512), multiply(1024), multiply(1536)], sums1)
+        sums0 = keep.tile([P, 512], F32)
+        nc.scalar.activation(sums0[:], multiply(0)[:], IDENTITY, bias=zero[:])
+        put_back(0, 512, sums0)
+        sums1 = keep.tile([P, 1024], F32)
+        scatter(512, [multiply(512), multiply(1024)], sums1)
+        held_bank = multiply(1536)
         late = turns.tile([P, 2048, 4], BF16, align_bytes=64, name="early")
         for s in (0, 1024, 1536, 512):
             spread(late[:, s : s + SPREAD, :], apart[2], s)
         for q in (3, 2):
             codes[q] = quantize(q, late[:, (q - 2) * QUANT : (q - 1) * QUANT, :])
+        held = turns.tile([P, 512], F32, align_bytes=64, name="apart2048")
+        scatter(1536, [held_bank], held)
+        for q in (3, 2):
             sums = keep.tile([P, SCAT], F32, name="sums%d" % q)
             scatter(q * SCAT, [multiply(q * SCAT), multiply(q * SCAT + BANK)], sums)
 

from contextlib import ExitStack

import concourse.mybir as mybir

K, T, E, C, N = 512, 4096, 16, 256, 128
FLOPS = 2 * K * N * E * C

F32 = mybir.dt.float32
BF16 = mybir.dt.bfloat16
U32 = mybir.dt.uint32
U16 = mybir.dt.uint16
U8 = mybir.dt.uint8
FP8X4 = mybir.dt.float8_e4m3fn_x4
MULT = mybir.AluOpType.mult
ADD = mybir.AluOpType.add
IDENTITY = mybir.ActivationFunctionType.Identity

P = 128
SLOTS = E * C
CHUNKS = (
    (
        (1024, ((512, False), (512, True))),
        (1024, ((512, False), (512, True))),
        (1024, ((512, False), (512, True))),
        (512, ((256, False), (256, True))),
        (512, ((256, False), (256, True))),
    ),
    (
        (1024, ((1024, False),)),
        (1024, ((1024, False),)),
        (1024, ((1024, False),)),
        (512, ((512, False),)),
        (512, ((512, True),)),
    ),
)
GATHERS = ((0, 1024), (1024, 1024), (2048, 2048))
QUANT = 1024
SPREAD = 512
WE = 4
SCAT = 1024
BANK = 512


def tile_routed_moe_kernel(tc, xT, w, gate, offs, out):
    nc = tc.nc
    with ExitStack() as ctx:
        keep = ctx.enter_context(tc.tile_pool(name="keep", bufs=1))
        rawp = ctx.enter_context(tc.tile_pool(name="rawp", bufs=6))
        turns = ctx.enter_context(tc.tile_pool(name="turns", bufs=1))
        psum = ctx.enter_context(tc.psum_pool(name="psum", bufs=8))

        offsets = keep.tile([P, SLOTS // 16], U16)
        nc.sync.dma_start(offsets[:], offs)

        pairs = [keep.tile([P, T, 2], BF16, align_bytes=64, name="pairs%d" % u) for u in (0, 1)]
        zero = turns.tile([P, 1], F32, align_bytes=64, name="early")
        nc.gpsimd.memset(zero[:], 0.0)
        apart = []
        for first, n in GATHERS:
            a = turns.tile([P, 2, n, 2], BF16, align_bytes=64, name="apart%d" % first)
            apart.append(a)
        planes = xT.rearrange("(p t) n -> p t n", t=4)
        for u in (0, 1):
            start = 0
            for width, pieces in CHUNKS[u]:
                raw = rawp.tile([P, 2, width], F32, name="raw")
                nc.sync.dma_start(raw[:], planes[:, 2 * u : 2 * u + 2, start : start + width])
                done = 0
                for n, on_vector in pieces:
                    dst = pairs[u][:, start + done : start + done + n, :]
                    src = raw[:, :, done : done + n].rearrange("p t n -> p n t")
                    if on_vector:
                        nc.vector.tensor_copy(dst, src)
                    else:
                        nc.scalar.copy(dst, src)
                    done += n
                start += width
            words = pairs[u][:].rearrange("p n t -> p (n t)").bitcast(U32)
            for (first, n), a in zip(GATHERS, apart):
                nc.vector.tensor_copy(
                    a[:, u, :, :].rearrange("p n i -> p (n i)").bitcast(U32),
                    words.indirect(offsets[:, first // 16 : (first + n) // 16]),
                )

        def spread(grouped, a, first):
            nc.scalar.copy(
                grouped.rearrange("p n (u i) -> p n u i", u=2),
                a[:, :, first : first + SPREAD, :].rearrange("p u n i -> p n u i"),
            )

        def quantize(q, grouped):
            cq = keep.tile([P, QUANT], U32, align_bytes=64, name="codes%d" % q)
            sq = keep.tile([P, QUANT], U8, align_bytes=64, name="scales%d" % q)
            nc.vector.quantize_mx(out=cq[:].bitcast(FP8X4), scales=sq[:], in_=grouped.rearrange("p n j -> p (n j)"))
            return cq, sq

        codes = {}
        for q in (0, 1):
            grouped = keep.tile([P, QUANT, 4], BF16, align_bytes=64, name="grouped%d" % q)
            for s in range(0, QUANT, SPREAD):
                spread(grouped[:, s : s + SPREAD, :], apart[q], s)
            codes[q] = quantize(q, grouped[:])

        wcodes = []
        wscales = []
        wst = turns.tile([P, E, N, 4], BF16, align_bytes=64, name="big")
        rows = w.rearrange("e (p j) n -> p e (j n)", j=4)
        for i in range(E // WE):
            raw = rawp.tile([P, WE, 4 * N], F32, name="raw")
            nc.sync.dma_start(raw[:], rows[:, i * WE : (i + 1) * WE, :])
            st = wst[:, i * WE : (i + 1) * WE, :, :]
            nc.gpsimd.tensor_scalar(st, raw[:].rearrange("p e (j n) -> p e n j", j=4), 1.0, 0.0, MULT, ADD)
            wc = keep.tile([P, WE * N], U32, align_bytes=64, name="wcodes%d" % i)
            ws = keep.tile([P, WE * N], U8, align_bytes=64, name="wscales%d" % i)
            nc.vector.quantize_mx(out=wc[:].bitcast(FP8X4), scales=ws[:], in_=st.rearrange("p e n j -> p (e n j)"))
            wcodes.append(wc)
            wscales.append(ws)

        gates = keep.tile([P, SLOTS], F32)
        for s in range(0, SLOTS, SCAT):
            nc.sync.dma_start(gates[:, s : s + SCAT], gate[:, s : s + SCAT])

        window = turns.tile([P, T], F32, align_bytes=64, name="big")

        def multiply(b):
            bank = psum.tile([P, BANK], F32)
            for slot in range(b, b + BANK, C):
                e, q, qo = slot // C, slot // QUANT, slot % QUANT
                wo = e % WE * N
                nc.tensor.matmul_mx(
                    out=bank[:, slot - b : slot - b + C],
                    lhsT=wcodes[e // WE][:, wo : wo + N].bitcast(FP8X4),
                    lhsT_scale=wscales[e // WE][:, wo : wo + N],
                    rhs=codes[q][0][:, qo : qo + C].bitcast(FP8X4),
                    rhs_scale=codes[q][1][:, qo : qo + C],
                    start=True,
                    stop=True,
                )
            return bank

        def scatter(start, banks, sums):
            for b, bank in enumerate(banks):
                nc.scalar.copy(sums[:, b * BANK : (b + 1) * BANK], bank[:])
            put_back(start, len(banks) * BANK, sums)

        def put_back(start, n, sums):
            idx = offsets[:, start // 16 : (start + n) // 16]
            nc.vector.tensor_tensor(window[:].indirect(idx), sums[:], gates[:, start : start + n], MULT)

        sums0 = keep.tile([P, 512], F32)
        nc.scalar.activation(sums0[:], multiply(0)[:], IDENTITY, bias=zero[:])
        put_back(0, 512, sums0)
        sums1 = keep.tile([P, 1024], F32)
        scatter(512, [multiply(512), multiply(1024)], sums1)
        held_bank = multiply(1536)
        late = turns.tile([P, 2048, 4], BF16, align_bytes=64, name="early")
        for s in (0, 1024, 1536, 512):
            spread(late[:, s : s + SPREAD, :], apart[2], s)
        for q in (3, 2):
            codes[q] = quantize(q, late[:, (q - 2) * QUANT : (q - 1) * QUANT, :])
        held = turns.tile([P, 512], F32, align_bytes=64, name="apart2048")
        scatter(1536, [held_bank], held)
        for q in (3, 2):
            sums = keep.tile([P, SCAT], F32, name="sums%d" % q)
            scatter(q * SCAT, [multiply(q * SCAT), multiply(q * SCAT + BANK)], sums)

        nc.sync.dma_start(out, window[:])
